import numpy as np
import ml_dtypes


def mxq(x, axis, fmt="e4m3"):
    dtype, down = {"e4m3": (ml_dtypes.float8_e4m3fn, 7), "e5m2": (ml_dtypes.float8_e5m2, 14)}[fmt]
    v = np.moveaxis(np.asarray(x, np.float32).astype(ml_dtypes.bfloat16).astype(np.float64), axis, -1)
    blocks = v.reshape(v.shape[:-1] + (-1, 32))
    amax = np.abs(blocks).max(-1, keepdims=True)
    byte = np.maximum(np.where(amax > 0, np.frexp(amax)[1] - 1 + 127, 0) - down, 1)
    scale = np.exp2(byte - 127.0)
    codes = (blocks / scale).astype(np.float32).astype(dtype).astype(np.float64)
    return np.moveaxis((codes * scale).reshape(v.shape), -1, axis)


WIDE = False


def mx_kscale(k):
    if not WIDE:
        return np.ones(k)
    levels = np.array([10, -10, 5, -5, 0])
    if k % 512:
        return np.exp2(np.random.permutation(np.resize(levels, k // 32))).repeat(32)
    a = np.empty((k // 512, 16))
    for p in range(k // 512):
        a[p, :8] = np.random.permutation(np.resize(levels, 8))
        for g in range(8):
            far = levels[np.abs(levels - a[p, g]) >= 10]
            a[p, g + 8] = far[np.random.randint(len(far))]
    return np.exp2(a.ravel()).repeat(32)


BF16 = ml_dtypes.bfloat16


def bf(x):
    return np.asarray(x, np.float32).astype(BF16)


def f64(x):
    return np.asarray(x).astype(np.float64)


E2M1 = np.array([0.0, 0.5, 1.0, 1.5, 2.0, 3.0, 4.0, 6.0, -0.0, -0.5, -1.0, -1.5, -2.0, -3.0, -4.0, -6.0])


def pack_weight(w, fmt):
    k, n = w.shape
    w = f64(bf(w)).reshape(k // 32, 32, n)
    amax = np.abs(w).max(1)
    if fmt == "e4m3":
        byte = np.frexp(amax)[1] - 1 + 127 - 7
    else:
        mant, ex = np.frexp(amax / 6.0)
        byte = np.where(mant > 0.5, ex, ex - 1) + 127
    byte = np.clip(np.where(amax > 0, byte, 1), 1, 254)
    scaled = (w * np.exp2(127.0 - byte)[:, None, :]).reshape(k, n).astype(np.float32)
    by_word = np.ascontiguousarray(scaled.reshape(k // 512, 128, 4, n).transpose(0, 1, 3, 2))
    if fmt == "e4m3":
        words = by_word.astype(ml_dtypes.float8_e4m3fn).view(np.uint8)
    else:
        c = by_word.astype(ml_dtypes.float4_e2m1fn).view(np.uint8) & 0xF
        words = c[..., 0::2] | (c[..., 1::2] << 4)
    return np.ascontiguousarray(words), np.ascontiguousarray(byte.astype(np.uint8).reshape(k // 512, 16, n))


def unpack_weight(words, scales, fmt):
    g, p, n, _ = words.shape
    if fmt == "e4m3":
        vals = np.ascontiguousarray(words).view(ml_dtypes.float8_e4m3fn).astype(np.float64)
    else:
        nib = np.empty((g, p, n, 4), np.uint8)
        nib[..., 0::2] = words & 0xF
        nib[..., 1::2] = words >> 4
        vals = E2M1[nib]
    vals = vals * np.repeat(np.exp2(scales.astype(np.float64) - 127.0), 8, axis=1)[..., None]
    return vals.transpose(0, 1, 3, 2).reshape(g * 512, n)
def pack4(w):
    words, scales = pack_weight(w, "e2m1")
    return words.reshape(words.shape[0], 128, -1), scales


def unpack4(words, scales):
    return unpack_weight(words.reshape(words.shape[0], 128, -1, 2), scales, "e2m1")


M, D, N, V = 1024, 1024, 2048, 1024
BETA = 0.7


def setup_inputs():
    s, t = mx_kscale(D), mx_kscale(N)
    z = np.random.standard_normal((D, M)) * np.sqrt(BETA / np.sqrt(D))
    x = np.random.standard_normal((D, N)) * np.sqrt(BETA / np.sqrt(D))
    u = np.exp((BETA * np.sqrt(D) - (x ** 2).sum(0)) / 2)
    a = np.exp((BETA * np.sqrt(D) - (z ** 2).sum(0)) / 2)
    offset = (np.arange(N)[:, None] - (N // V) * np.arange(V)[None, :]) % N
    c = np.where(offset < N // 2, 1.0, -1.0) * np.abs(np.random.standard_normal((N, V))) / np.sqrt(N)
    z_words, z_scales = pack4(z * s[:, None])
    x_words, x_scales = pack4(x / s[:, None])
    c_words, c_scales = pack_weight(c / t[:, None], "e4m3")
    return {"z_words": z_words, "z_scales": z_scales,
            "x_words": x_words, "x_scales": x_scales,
            "c_words": c_words, "c_scales": c_scales,
            "u": bf(u * t), "a": bf(a),
            "r": bf((1 + 0.1 * np.random.standard_normal(V)) / M)}


def reference(z_words, z_scales, x_words, x_scales, c_words, c_scales, u, a, r):
    z = unpack4(z_words, z_scales)
    x = unpack4(x_words, x_scales)
    c = unpack_weight(c_words, c_scales, "e4m3")
    p = z.T @ x
    h = np.exp(p) * f64(u)[None, :]
    w = (mxq(h, 1, "e4m3") @ c) * f64(a)[:, None]
    stat = (w ** 2).sum(0) * f64(r)
    return w, stat

@@ -1,0 +1,269 @@
+from contextlib import ExitStack
+
+import concourse.mybir as mybir
+
+F32 = mybir.dt.float32
+BF16 = mybir.dt.bfloat16
+I32 = mybir.dt.int32
+U32 = mybir.dt.uint32
+U8 = mybir.dt.uint8
+FP8X4 = mybir.dt.float8_e4m3fn_x4
+FP4X4 = mybir.dt.float4_e2m1fn_x4
+ACT = mybir.ActivationFunctionType
+ALU = mybir.AluOpType
+
+P = 128
+D, M, N, V = 1024, 1024, 2048, 1024
+GROUPS = N // 512
+KD = D // 512
+CHUNKS = [(0, 512), (512, 256), (768, 256)]
+BANK = 512
+FLOPS = 2 * D * M * N + 2 * M * N * V
+
+
+def tile_kernel_change_scan_s4_kernel(
+    tc, z_words, z_scales, x_words, x_scales, c_words, c_scales, u, a, r, out_0, out_1
+):
+    nc = tc.nc
+    with ExitStack() as ctx:
+        ctx.enter_context(nc.allow_non_contiguous_dma("small vectors"))
+        keep = ctx.enter_context(tc.tile_pool(name="keep", bufs=1))
+        work = ctx.enter_context(tc.tile_pool(name="work", bufs=3))
+        psum = ctx.enter_context(tc.psum_pool(name="psum", bufs=4))
+        ctx.enter_context(tc.manual_schedule())
+
+        x_raw = [keep.tile([P, KD, 1024], U8, name=f"x_raw{g}", align_bytes=256) for g in range(GROUPS)]
+        x_perm = [keep.tile([P, KD, 4, 256], U8, name=f"x_perm{g}", align_bytes=256) for g in range(GROUPS)]
+        xs_raw = keep.tile([P, KD, N], U8, name="xs_raw", align_bytes=256)
+        xs_perm = [keep.tile([P, KD, 4, P], U8, name=f"xs_perm{g}", align_bytes=256) for g in range(GROUPS)]
+        z_sb = [keep.tile([P, KD, 1024], U8, name=f"z_sb{h}", align_bytes=256) for h in range(2)]
+        zs_sb = keep.tile([P, KD, M], U8, name="zs_sb", align_bytes=256)
+        c_sb = [keep.tile([P, 4 * V], U8, name=f"c_sb{g}", align_bytes=256) for g in range(GROUPS)]
+        cs_sb = keep.tile([P, V], U8, name="cs_sb", align_bytes=256)
+        u_sb = keep.tile([P, GROUPS * 4], BF16, name="u_sb")
+        a_bf = keep.tile([P, M // P], BF16, name="a_bf")
+        a_sb = keep.tile([P, M // P], F32, name="a_sb")
+        r_sb = keep.tile([1, V], BF16, name="r_sb")
+        ones = keep.tile([P, P], F32, name="ones")
+        acc = keep.tile([P, V], F32, name="acc")
+        stat_sb = keep.tile([1, V], F32, name="stat_sb")
+        h_codes = [
+            [keep.tile([P, n], U32, name=f"h_codes{c}_{g}", align_bytes=256) for g in range(GROUPS)]
+            for c, (m0, n) in enumerate(CHUNKS)
+        ]
+        h_scales = [
+            [keep.tile([P, n], U8, name=f"h_scales{c}_{g}", align_bytes=256) for g in range(GROUPS)]
+            for c, (m0, n) in enumerate(CHUNKS)
+        ]
+
+        def load_x(g):
+            nc.sync.dma_start(
+                out=x_raw[g][:],
+                in_=x_words[:, :, 1024 * g : 1024 * (g + 1)].rearrange("d p b -> p d b"),
+            )
+
+        def load_z(h):
+            nc.sync.dma_start(
+                out=z_sb[h][:],
+                in_=z_words[:, :, 1024 * h : 1024 * (h + 1)].rearrange("d p b -> p d b"),
+            )
+
+        def load_scales(eng, tile, dram, q):
+            eng.dma_start(
+                out=tile[32 * q : 32 * q + 4, :, :].bitcast(I32),
+                in_=dram[:, 4 * q : 4 * q + 4, :].bitcast(I32).rearrange("d r n -> r d n"),
+            )
+
+        nc.vector.memset(xs_raw[:].rearrange("p d n -> p (d n)").bitcast(I32), 0)
+        nc.vector.memset(zs_sb[:].rearrange("p d n -> p (d n)").bitcast(I32), 0)
+        nc.vector.memset(cs_sb[:].bitcast(I32), 0)
+
+        load_x(0)
+        load_z(0)
+        for q in range(4):
+            load_scales(nc.sync, xs_raw, x_scales, q)
+        load_scales(nc.sync, zs_sb, z_scales, 0)
+        load_scales(nc.sync, zs_sb, z_scales, 1)
+        load_scales(nc.gpsimd, zs_sb, z_scales, 2)
+        load_scales(nc.gpsimd, zs_sb, z_scales, 3)
+        nc.gpsimd.dma_start(
+            out=u_sb[:].rearrange("p (g t) -> p g t", t=4),
+            in_=u.rearrange("(g p t) -> p g t", p=P, t=4),
+        )
+        nc.gpsimd.dma_start(out=a_bf[:], in_=a.rearrange("(k p) -> p k", p=P))
+        nc.gpsimd.dma_start(out=r_sb[:], in_=r.unsqueeze(0))
+        nc.gpsimd.memset(ones[:], 1.0)
+        load_x(1)
+        load_x(2)
+        load_x(3)
+        load_z(1)
+        for q in range(4):
+            nc.sync.dma_start(
+                out=cs_sb[32 * q : 32 * q + 16, :].bitcast(I32),
+                in_=c_scales[:, 4 * q : 4 * q + 4, :].bitcast(I32),
+            )
+        for g in range(GROUPS):
+            nc.sync.dma_start(out=c_sb[g][:], in_=c_words[g].rearrange("p n t -> p (n t)"))
+
+        def permute(g):
+            for d in range(KD):
+                nc.vector.tensor_copy(
+                    out=x_perm[g][:, d, :, :].rearrange("p t (m b) -> p t m b", b=2),
+                    in_=x_raw[g][:, d, :].rearrange("p (m t b) -> p t m b", t=4, b=2),
+                )
+            nc.vector.tensor_copy(
+                out=xs_perm[g][:],
+                in_=xs_raw[:, :, 512 * g : 512 * (g + 1)].rearrange("p d (m t) -> p d t m", t=4),
+            )
+
+        e_tiles = {}
+        hb_tiles = {}
+
+        def stage1(c, g):
+            m0, n = CHUNKS[c]
+            h, zoff = m0 // 512, m0 % 512
+            per_bank = BANK // n
+            e = work.tile([P, 4, n], F32, name=f"e{c}_{g}", tag="e", bufs=8)
+            e_tiles[c, g] = e
+            for t0 in range(0, 4, per_bank):
+                ps = psum.tile([P, per_bank, n], F32, name=f"p{c}_{g}_{t0}", tag="p", bufs=4)
+                for i in range(per_bank):
+                    for d in range(KD):
+                        nc.tensor.matmul_mx(
+                            out=ps[:, i, :],
+                            lhsT=x_perm[g][:, d, t0 + i, :].bitcast(FP4X4),
+                            lhsT_scale=xs_perm[g][:, d, t0 + i, :],
+                            rhs=z_sb[h][:, d, 2 * zoff : 2 * (zoff + n)].bitcast(FP4X4),
+                            rhs_scale=zs_sb[:, d, m0 : m0 + n],
+                            start=(d == 0),
+                            stop=(d == KD - 1),
+                        )
+                nc.scalar.activation(out=e[:, t0 : t0 + per_bank, :], in_=ps[:], func=ACT.Exp)
+
+        def scale_by_u(c, g):
+            m0, n = CHUNKS[c]
+            hb = work.tile([P, n, 4], BF16, name=f"hb{c}_{g}", tag="hb", bufs=3, align_bytes=256)
+            hb_tiles[c, g] = hb
+            nc.vector.tensor_tensor(
+                out=hb[:],
+                in0=e_tiles[c, g][:].rearrange("p t m -> p m t"),
+                in1=u_sb[:, 4 * g : 4 * (g + 1)].unsqueeze(1).to_broadcast([P, n, 4]),
+                op=ALU.mult,
+            )
+
+        def quantize(c, g):
+            nc.vector.quantize_mx(
+                out=h_codes[c][g][:].bitcast(FP8X4),
+                scales=h_scales[c][g][:],
+                in_=hb_tiles[c, g][:].rearrange("p m t -> p (m t)"),
+            )
+
+        tiles = []
+        for c, (m0, n) in enumerate(CHUNKS):
+            for j in range(n // P):
+                tiles.append((c, j))
+        last = len(tiles) - 1
+        halves = [(0, 512), (512, 1024)]
+        sq_tiles = {}
+        y_tiles = {}
+
+        def product(k, c0, c1):
+            c, j = tiles[k]
+            ps = psum.tile([P, c1 - c0], F32, name=f"y{k}_{c0}", tag="y", bufs=4)
+            y_tiles[k, c0] = ps
+            for g in range(GROUPS):
+                nc.tensor.matmul_mx(
+                    out=ps[:],
+                    lhsT=h_codes[c][g][:, P * j : P * (j + 1)].bitcast(FP8X4),
+                    lhsT_scale=h_scales[c][g][:, P * j : P * (j + 1)],
+                    rhs=c_sb[g][:, 4 * c0 : 4 * c1].bitcast(FP8X4),
+                    rhs_scale=cs_sb[4 * g : P, c0:c1],
+                    start=(g == 0),
+                    stop=(g == GROUPS - 1),
+                )
+
+        def square(k, c0, c1):
+            if k not in sq_tiles:
+                sq_tiles[k] = acc if k == 0 else work.tile([P, V], F32, name=f"sq{k}", tag="sq", bufs=5)
+            nc.scalar.activation(
+                out=sq_tiles[k][:, c0:c1], in_=y_tiles[k, c0][:], func=ACT.Square, scale=a_sb[:, k : k + 1]
+            )
+
+        def accumulate(k, c0, c1):
+            nc.vector.tensor_tensor(out=acc[:, c0:c1], in0=acc[:, c0:c1], in1=sq_tiles[k][:, c0:c1], op=ALU.add)
+
+        def contrast_vector(k, c0, c1):
+            w = work.tile([P, c1 - c0], F32, name=f"wv{k}_{c0}", tag="wv", bufs=5)
+            nc.vector.tensor_scalar(
+                out=w[:], in0=y_tiles[k, c0][:], scalar1=a_sb[:, k : k + 1], scalar2=None, op0=ALU.mult
+            )
+            nc.sync.dma_start(out=out_0[P * k : P * (k + 1), c0:c1], in_=w[:])
+
+        def stage2(k):
+            w = work.tile([P, V], F32, name=f"w{k}", tag="w", bufs=4)
+            for c0, c1 in halves:
+                product(k, c0, c1)
+                square(k, c0, c1)
+                nc.scalar.activation(out=w[:, c0:c1], in_=y_tiles[k, c0][:], func=ACT.Copy, scale=a_sb[:, k : k + 1])
+            nc.sync.dma_start(out=out_0[P * k : P * (k + 1), :], in_=w[:])
+
+        def add_both(k):
+            for c0, c1 in halves:
+                accumulate(k, c0, c1)
+
+        def finish(c0, c1, sources):
+            ps = psum.tile([P, c1 - c0], F32, name=f"stat{c0}", tag="p", bufs=4)
+            for i, s in enumerate(sources):
+                nc.tensor.matmul(
+                    out=ps[:], lhsT=ones[:], rhs=s[:, c0:c1], start=(i == 0), stop=(i == len(sources) - 1)
+                )
+            return ps
+
+        def store_stat(c0, c1, ps):
+            nc.vector.tensor_tensor(out=stat_sb[:, c0:c1], in0=ps[0:1, :], in1=r_sb[:, c0:c1], op=ALU.mult)
+            nc.sync.dma_start(out=out_1.unsqueeze(0)[:, c0:c1], in_=stat_sb[:, c0:c1])
+
+        units = [(c, g) for c in range(len(CHUNKS)) for g in range(GROUPS)]
+        for g in range(GROUPS):
+            permute(g)
+            stage1(*units[g])
+        for i in range(len(units)):
+            if i + 4 < len(units):
+                stage1(*units[i + 4])
+            if i == 3:
+                nc.vector.tensor_copy(out=a_sb[:], in_=a_bf[:])
+            if i == 9:
+                stage2(0)
+                stage2(1)
+            scale_by_u(*units[i])
+            if i:
+                quantize(*units[i - 1])
+            if i >= 9:
+                add_both(i - 8)
+                stage2(i - 7)
+        quantize(*units[-1])
+        stage2(5)
+        add_both(4)
+        add_both(5)
+        product(6, 0, 512)
+        square(6, 0, 512)
+        accumulate(6, 0, 512)
+        contrast_vector(6, 0, 512)
+        product(7, 0, 512)
+        square(7, 0, 512)
+        accumulate(7, 0, 512)
+        contrast_vector(7, 0, 512)
+        product(6, 512, 1024)
+        square(6, 512, 1024)
+        accumulate(6, 512, 1024)
+        contrast_vector(6, 512, 1024)
+        for c0, c1 in ((512, 768), (768, 1024)):
+            product(7, c0, c1)
+            square(7, c0, c1)
+            contrast_vector(7, c0, c1)
+        ps_a = finish(0, 512, [acc])
+        ps_b = finish(512, 768, [acc, sq_tiles[7]])
+        ps_c = finish(768, 1024, [acc, sq_tiles[7]])
+        store_stat(0, 512, ps_a)
+        store_stat(512, 768, ps_b)
+        store_stat(768, 1024, ps_c)

@@ -16,8 +16,9 @@ P = 128
 D, M, N, V = 1024, 1024, 2048, 1024
 GROUPS = N // 512
 KD = D // 512
-CHUNKS = [(0, 512), (512, 256), (768, 256)]
+CHUNKS = [(0, 256), (256, 512), (768, 256)]
 BANK = 512
+WARM = 14
 FLOPS = 2 * D * M * N + 2 * M * N * V
 
 
@@ -34,10 +35,12 @@ def tile_kernel_change_scan_s4_kernel(
 
         x_raw = [keep.tile([P, KD, 1024], U8, name=f"x_raw{g}", align_bytes=256) for g in range(GROUPS)]
         x_perm = [keep.tile([P, KD, 4, 256], U8, name=f"x_perm{g}", align_bytes=256) for g in range(GROUPS)]
-        xs_raw = keep.tile([P, KD, N], U8, name="xs_raw", align_bytes=256)
-        xs_perm = [keep.tile([P, KD, 4, P], U8, name=f"xs_perm{g}", align_bytes=256) for g in range(GROUPS)]
-        z_sb = [keep.tile([P, KD, 1024], U8, name=f"z_sb{h}", align_bytes=256) for h in range(2)]
+        xs_raw = keep.tile([P, 512], U8, name="xs_raw", align_bytes=256)
+        xs_perm = keep.tile([P, 512], U8, name="xs_perm", align_bytes=256)
+        xs_sb = keep.tile([P, KD, N], U8, name="xs_sb", align_bytes=256)
+        z_sb = [keep.tile([P, KD, 2 * n], U8, name=f"z_sb{c}", align_bytes=256) for c, (m0, n) in enumerate(CHUNKS)]
         zs_sb = keep.tile([P, KD, M], U8, name="zs_sb", align_bytes=256)
+        warm = keep.tile([P, BANK], BF16, name="warm")
         c_sb = [keep.tile([P, 4 * V], U8, name=f"c_sb{g}", align_bytes=256) for g in range(GROUPS)]
         cs_sb = keep.tile([P, V], U8, name="cs_sb", align_bytes=256)
         u_sb = keep.tile([P, GROUPS * 4], BF16, name="u_sb")
@@ -56,47 +59,46 @@ def tile_kernel_change_scan_s4_kernel(
             for c, (m0, n) in enumerate(CHUNKS)
         ]
 
-        def load_x(g):
-            nc.sync.dma_start(
-                out=x_raw[g][:],
-                in_=x_words[:, :, 1024 * g : 1024 * (g + 1)].rearrange("d p b -> p d b"),
-            )
+        def load_words(tile, dram, b0, b1):
+            nc.sync.dma_start(out=tile[:], in_=dram[:, :, b0:b1].rearrange("d p b -> p d b"))
 
-        def load_z(h):
-            nc.sync.dma_start(
-                out=z_sb[h][:],
-                in_=z_words[:, :, 1024 * h : 1024 * (h + 1)].rearrange("d p b -> p d b"),
-            )
-
-        def load_scales(eng, tile, dram, q):
-            eng.dma_start(
-                out=tile[32 * q : 32 * q + 4, :, :].bitcast(I32),
-                in_=dram[:, 4 * q : 4 * q + 4, :].bitcast(I32).rearrange("d r n -> r d n"),
-            )
-
-        nc.vector.memset(xs_raw[:].rearrange("p d n -> p (d n)").bitcast(I32), 0)
-        nc.vector.memset(zs_sb[:].rearrange("p d n -> p (d n)").bitcast(I32), 0)
-        nc.vector.memset(cs_sb[:].bitcast(I32), 0)
-
-        load_x(0)
-        load_z(0)
-        for q in range(4):
-            load_scales(nc.sync, xs_raw, x_scales, q)
-        load_scales(nc.sync, zs_sb, z_scales, 0)
-        load_scales(nc.sync, zs_sb, z_scales, 1)
-        load_scales(nc.gpsimd, zs_sb, z_scales, 2)
-        load_scales(nc.gpsimd, zs_sb, z_scales, 3)
         nc.gpsimd.dma_start(
             out=u_sb[:].rearrange("p (g t) -> p g t", t=4),
             in_=u.rearrange("(g p t) -> p g t", p=P, t=4),
         )
+        nc.gpsimd.memset(xs_sb[:].rearrange("p d n -> p (d n)").bitcast(I32), 0)
         nc.gpsimd.dma_start(out=a_bf[:], in_=a.rearrange("(k p) -> p k", p=P))
+        nc.gpsimd.memset(cs_sb[:].bitcast(I32), 0)
         nc.gpsimd.dma_start(out=r_sb[:], in_=r.unsqueeze(0))
         nc.gpsimd.memset(ones[:], 1.0)
-        load_x(1)
-        load_x(2)
-        load_x(3)
-        load_z(1)
+        nc.vector.memset(zs_sb[:].rearrange("p d n -> p (d n)").bitcast(I32), 0)
+        nc.vector.memset(warm[:], 0.0)
+
+        nc.sync.dma_start(
+            out=xs_raw[:].bitcast(I32),
+            in_=x_scales.bitcast(I32).rearrange("d q (g n) -> (d q g) n", g=GROUPS),
+        )
+        load_words(x_raw[0], x_words, 0, 1024)
+        for q in range(4):
+            nc.sync.dma_start(
+                out=zs_sb[32 * q : 32 * q + 4, :, :].bitcast(I32),
+                in_=z_scales[:, 4 * q : 4 * q + 4, :].bitcast(I32).rearrange("d r n -> r d n"),
+            )
+        load_words(z_sb[0], z_words, 0, 2 * CHUNKS[0][1])
+        load_words(x_raw[1], x_words, 1024, 2048)
+        nc.vector.tensor_copy(
+            out=xs_perm[:].rearrange("p (t m) -> p t m", t=4), in_=xs_raw[:].rearrange("p (m t) -> p t m", t=4)
+        )
+        for d in range(KD):
+            for q in range(4):
+                nc.sync.dma_start(
+                    out=xs_sb[32 * q : 32 * q + 4, d, :].bitcast(I32),
+                    in_=xs_perm[64 * d + 16 * q : 64 * d + 16 * (q + 1), :].bitcast(I32),
+                )
+        load_words(x_raw[2], x_words, 2048, 3072)
+        load_words(x_raw[3], x_words, 3072, 4096)
+        for c in (1, 2):
+            load_words(z_sb[c], z_words, 2 * CHUNKS[c][0], 2 * (CHUNKS[c][0] + CHUNKS[c][1]))
         for q in range(4):
             nc.sync.dma_start(
                 out=cs_sb[32 * q : 32 * q + 16, :].bitcast(I32),
@@ -105,23 +107,22 @@ def tile_kernel_change_scan_s4_kernel(
         for g in range(GROUPS):
             nc.sync.dma_start(out=c_sb[g][:], in_=c_words[g].rearrange("p n t -> p (n t)"))
 
+        warm_ps = psum.tile([P, BANK], F32, name="warm_ps", tag="p", bufs=4)
+        for i in range(WARM):
+            nc.tensor.matmul(out=warm_ps[:], lhsT=warm[:, 0:P], rhs=warm[:], start=True, stop=True)
+
         def permute(g):
             for d in range(KD):
                 nc.vector.tensor_copy(
                     out=x_perm[g][:, d, :, :].rearrange("p t (m b) -> p t m b", b=2),
                     in_=x_raw[g][:, d, :].rearrange("p (m t b) -> p t m b", t=4, b=2),
                 )
-            nc.vector.tensor_copy(
-                out=xs_perm[g][:],
-                in_=xs_raw[:, :, 512 * g : 512 * (g + 1)].rearrange("p d (m t) -> p d t m", t=4),
-            )
 
         e_tiles = {}
         hb_tiles = {}
 
         def stage1(c, g):
             m0, n = CHUNKS[c]
-            h, zoff = m0 // 512, m0 % 512
             per_bank = BANK // n
             e = work.tile([P, 4, n], F32, name=f"e{c}_{g}", tag="e", bufs=8)
             e_tiles[c, g] = e
@@ -132,8 +133,8 @@ def tile_kernel_change_scan_s4_kernel(
                         nc.tensor.matmul_mx(
                             out=ps[:, i, :],
                             lhsT=x_perm[g][:, d, t0 + i, :].bitcast(FP4X4),
-                            lhsT_scale=xs_perm[g][:, d, t0 + i, :],
-                            rhs=z_sb[h][:, d, 2 * zoff : 2 * (zoff + n)].bitcast(FP4X4),
+                            lhsT_scale=xs_sb[:, d, 512 * g + P * (t0 + i) : 512 * g + P * (t0 + i + 1)],
+                            rhs=z_sb[c][:, d, :].bitcast(FP4X4),
                             rhs_scale=zs_sb[:, d, m0 : m0 + n],
                             start=(d == 0),
                             stop=(d == KD - 1),
@@ -145,9 +146,9 @@ def tile_kernel_change_scan_s4_kernel(
             hb = work.tile([P, n, 4], BF16, name=f"hb{c}_{g}", tag="hb", bufs=3, align_bytes=256)
             hb_tiles[c, g] = hb
             nc.vector.tensor_tensor(
-                out=hb[:],
-                in0=e_tiles[c, g][:].rearrange("p t m -> p m t"),
-                in1=u_sb[:, 4 * g : 4 * (g + 1)].unsqueeze(1).to_broadcast([P, n, 4]),
+                out=hb[:].rearrange("p (c i) t -> p c t i", i=4),
+                in0=e_tiles[c, g][:].rearrange("p t (c i) -> p c t i", i=4),
+                in1=u_sb[:, 4 * g : 4 * (g + 1)].unsqueeze(1).unsqueeze(3).to_broadcast([P, n // 4, 4, 4]),
                 op=ALU.mult,
             )
 
@@ -207,6 +208,13 @@ def tile_kernel_change_scan_s4_kernel(
                 nc.scalar.activation(out=w[:, c0:c1], in_=y_tiles[k, c0][:], func=ACT.Copy, scale=a_sb[:, k : k + 1])
             nc.sync.dma_start(out=out_0[P * k : P * (k + 1), :], in_=w[:])
 
+        def stage2_half(k, c0, c1):
+            product(k, c0, c1)
+            square(k, c0, c1)
+            w = work.tile([P, c1 - c0], F32, name=f"wh{k}_{c0}", tag="wv", bufs=5)
+            nc.scalar.activation(out=w[:], in_=y_tiles[k, c0][:], func=ACT.Copy, scale=a_sb[:, k : k + 1])
+            nc.sync.dma_start(out=out_0[P * k : P * (k + 1), c0:c1], in_=w[:])
+
         def add_both(k):
             for c0, c1 in halves:
                 accumulate(k, c0, c1)
@@ -232,7 +240,7 @@ def tile_kernel_change_scan_s4_kernel(
                 stage1(*units[i + 4])
             if i == 3:
                 nc.vector.tensor_copy(out=a_sb[:], in_=a_bf[:])
-            if i == 9:
+            if i == 8:
                 stage2(0)
                 stage2(1)
             scale_by_u(*units[i])
@@ -260,10 +268,9 @@ def tile_kernel_change_scan_s4_kernel(
         for c0, c1 in ((512, 768), (768, 1024)):
             product(7, c0, c1)
             square(7, c0, c1)
+            accumulate(7, c0, c1)
             contrast_vector(7, c0, c1)
-        ps_a = finish(0, 512, [acc])
-        ps_b = finish(512, 768, [acc, sq_tiles[7]])
-        ps_c = finish(768, 1024, [acc, sq_tiles[7]])
-        store_stat(0, 512, ps_a)
-        store_stat(512, 768, ps_b)
-        store_stat(768, 1024, ps_c)
+        ends = [(0, 512), (512, 768), (768, 1024)]
+        sums = [finish(c0, c1, [acc]) for c0, c1 in ends]
+        for (c0, c1), ps in zip(ends, sums):
+            store_stat(c0, c1, ps)

from contextlib import ExitStack

import concourse.mybir as mybir

F32 = mybir.dt.float32
BF16 = mybir.dt.bfloat16
I32 = mybir.dt.int32
U32 = mybir.dt.uint32
U8 = mybir.dt.uint8
FP8X4 = mybir.dt.float8_e4m3fn_x4
FP4X4 = mybir.dt.float4_e2m1fn_x4
ACT = mybir.ActivationFunctionType
ALU = mybir.AluOpType

P = 128
D, M, N, V = 1024, 1024, 2048, 1024
GROUPS = N // 512
KD = D // 512
CHUNKS = [(0, 256), (256, 512), (768, 256)]
BANK = 512
WARM = 14
FLOPS = 2 * D * M * N + 2 * M * N * V


def tile_kernel_change_scan_s4_kernel(
    tc, z_words, z_scales, x_words, x_scales, c_words, c_scales, u, a, r, out_0, out_1
):
    nc = tc.nc
    with ExitStack() as ctx:
        ctx.enter_context(nc.allow_non_contiguous_dma("small vectors"))
        keep = ctx.enter_context(tc.tile_pool(name="keep", bufs=1))
        work = ctx.enter_context(tc.tile_pool(name="work", bufs=3))
        psum = ctx.enter_context(tc.psum_pool(name="psum", bufs=4))
        ctx.enter_context(tc.manual_schedule())

        x_raw = [keep.tile([P, KD, 1024], U8, name=f"x_raw{g}", align_bytes=256) for g in range(GROUPS)]
        x_perm = [keep.tile([P, KD, 4, 256], U8, name=f"x_perm{g}", align_bytes=256) for g in range(GROUPS)]
        xs_raw = keep.tile([P, 512], U8, name="xs_raw", align_bytes=256)
        xs_perm = keep.tile([P, 512], U8, name="xs_perm", align_bytes=256)
        xs_sb = keep.tile([P, KD, N], U8, name="xs_sb", align_bytes=256)
        z_sb = [keep.tile([P, KD, 2 * n], U8, name=f"z_sb{c}", align_bytes=256) for c, (m0, n) in enumerate(CHUNKS)]
        zs_sb = keep.tile([P, KD, M], U8, name="zs_sb", align_bytes=256)
        warm = keep.tile([P, BANK], BF16, name="warm")
        c_sb = [keep.tile([P, 4 * V], U8, name=f"c_sb{g}", align_bytes=256) for g in range(GROUPS)]
        cs_sb = keep.tile([P, V], U8, name="cs_sb", align_bytes=256)
        u_sb = keep.tile([P, GROUPS * 4], BF16, name="u_sb")
        a_bf = keep.tile([P, M // P], BF16, name="a_bf")
        a_sb = keep.tile([P, M // P], F32, name="a_sb")
        r_sb = keep.tile([1, V], BF16, name="r_sb")
        ones = keep.tile([P, P], F32, name="ones")
        acc = keep.tile([P, V], F32, name="acc")
        stat_sb = keep.tile([1, V], F32, name="stat_sb")
        h_codes = [
            [keep.tile([P, n], U32, name=f"h_codes{c}_{g}", align_bytes=256) for g in range(GROUPS)]
            for c, (m0, n) in enumerate(CHUNKS)
        ]
        h_scales = [
            [keep.tile([P, n], U8, name=f"h_scales{c}_{g}", align_bytes=256) for g in range(GROUPS)]
            for c, (m0, n) in enumerate(CHUNKS)
        ]

        def load_words(tile, dram, b0, b1):
            nc.sync.dma_start(out=tile[:], in_=dram[:, :, b0:b1].rearrange("d p b -> p d b"))

        nc.gpsimd.dma_start(
            out=u_sb[:].rearrange("p (g t) -> p g t", t=4),
            in_=u.rearrange("(g p t) -> p g t", p=P, t=4),
        )
        nc.gpsimd.memset(xs_sb[:].rearrange("p d n -> p (d n)").bitcast(I32), 0)
        nc.gpsimd.dma_start(out=a_bf[:], in_=a.rearrange("(k p) -> p k", p=P))
        nc.gpsimd.memset(cs_sb[:].bitcast(I32), 0)
        nc.gpsimd.dma_start(out=r_sb[:], in_=r.unsqueeze(0))
        nc.gpsimd.memset(ones[:], 1.0)
        nc.vector.memset(zs_sb[:].rearrange("p d n -> p (d n)").bitcast(I32), 0)
        nc.vector.memset(warm[:], 0.0)

        nc.sync.dma_start(
            out=xs_raw[:].bitcast(I32),
            in_=x_scales.bitcast(I32).rearrange("d q (g n) -> (d q g) n", g=GROUPS),
        )
        load_words(x_raw[0], x_words, 0, 1024)
        for q in range(4):
            nc.sync.dma_start(
                out=zs_sb[32 * q : 32 * q + 4, :, :].bitcast(I32),
                in_=z_scales[:, 4 * q : 4 * q + 4, :].bitcast(I32).rearrange("d r n -> r d n"),
            )
        load_words(z_sb[0], z_words, 0, 2 * CHUNKS[0][1])
        load_words(x_raw[1], x_words, 1024, 2048)
        nc.vector.tensor_copy(
            out=xs_perm[:].rearrange("p (t m) -> p t m", t=4), in_=xs_raw[:].rearrange("p (m t) -> p t m", t=4)
        )
        for d in range(KD):
            for q in range(4):
                nc.sync.dma_start(
                    out=xs_sb[32 * q : 32 * q + 4, d, :].bitcast(I32),
                    in_=xs_perm[64 * d + 16 * q : 64 * d + 16 * (q + 1), :].bitcast(I32),
                )
        load_words(x_raw[2], x_words, 2048, 3072)
        load_words(x_raw[3], x_words, 3072, 4096)
        for c in (1, 2):
            load_words(z_sb[c], z_words, 2 * CHUNKS[c][0], 2 * (CHUNKS[c][0] + CHUNKS[c][1]))
        for q in range(4):
            nc.sync.dma_start(
                out=cs_sb[32 * q : 32 * q + 16, :].bitcast(I32),
                in_=c_scales[:, 4 * q : 4 * q + 4, :].bitcast(I32),
            )
        for g in range(GROUPS):
            nc.sync.dma_start(out=c_sb[g][:], in_=c_words[g].rearrange("p n t -> p (n t)"))

        warm_ps = psum.tile([P, BANK], F32, name="warm_ps", tag="p", bufs=4)
        for i in range(WARM):
            nc.tensor.matmul(out=warm_ps[:], lhsT=warm[:, 0:P], rhs=warm[:], start=True, stop=True)

        def permute(g):
            for d in range(KD):
                nc.vector.tensor_copy(
                    out=x_perm[g][:, d, :, :].rearrange("p t (m b) -> p t m b", b=2),
                    in_=x_raw[g][:, d, :].rearrange("p (m t b) -> p t m b", t=4, b=2),
                )

        e_tiles = {}
        hb_tiles = {}

        def stage1(c, g):
            m0, n = CHUNKS[c]
            per_bank = BANK // n
            e = work.tile([P, 4, n], F32, name=f"e{c}_{g}", tag="e", bufs=8)
            e_tiles[c, g] = e
            for t0 in range(0, 4, per_bank):
                ps = psum.tile([P, per_bank, n], F32, name=f"p{c}_{g}_{t0}", tag="p", bufs=4)
                for i in range(per_bank):
                    for d in range(KD):
                        nc.tensor.matmul_mx(
                            out=ps[:, i, :],
                            lhsT=x_perm[g][:, d, t0 + i, :].bitcast(FP4X4),
                            lhsT_scale=xs_sb[:, d, 512 * g + P * (t0 + i) : 512 * g + P * (t0 + i + 1)],
                            rhs=z_sb[c][:, d, :].bitcast(FP4X4),
                            rhs_scale=zs_sb[:, d, m0 : m0 + n],
                            start=(d == 0),
                            stop=(d == KD - 1),
                        )
                nc.scalar.activation(out=e[:, t0 : t0 + per_bank, :], in_=ps[:], func=ACT.Exp)

        def scale_by_u(c, g):
            m0, n = CHUNKS[c]
            hb = work.tile([P, n, 4], BF16, name=f"hb{c}_{g}", tag="hb", bufs=3, align_bytes=256)
            hb_tiles[c, g] = hb
            nc.vector.tensor_tensor(
                out=hb[:].rearrange("p (c i) t -> p c t i", i=4),
                in0=e_tiles[c, g][:].rearrange("p t (c i) -> p c t i", i=4),
                in1=u_sb[:, 4 * g : 4 * (g + 1)].unsqueeze(1).unsqueeze(3).to_broadcast([P, n // 4, 4, 4]),
                op=ALU.mult,
            )

        def quantize(c, g):
            nc.vector.quantize_mx(
                out=h_codes[c][g][:].bitcast(FP8X4),
                scales=h_scales[c][g][:],
                in_=hb_tiles[c, g][:].rearrange("p m t -> p (m t)"),
            )

        tiles = []
        for c, (m0, n) in enumerate(CHUNKS):
            for j in range(n // P):
                tiles.append((c, j))
        last = len(tiles) - 1
        halves = [(0, 512), (512, 1024)]
        sq_tiles = {}
        y_tiles = {}

        def product(k, c0, c1):
            c, j = tiles[k]
            ps = psum.tile([P, c1 - c0], F32, name=f"y{k}_{c0}", tag="y", bufs=4)
            y_tiles[k, c0] = ps
            for g in range(GROUPS):
                nc.tensor.matmul_mx(
                    out=ps[:],
                    lhsT=h_codes[c][g][:, P * j : P * (j + 1)].bitcast(FP8X4),
                    lhsT_scale=h_scales[c][g][:, P * j : P * (j + 1)],
                    rhs=c_sb[g][:, 4 * c0 : 4 * c1].bitcast(FP8X4),
                    rhs_scale=cs_sb[4 * g : P, c0:c1],
                    start=(g == 0),
                    stop=(g == GROUPS - 1),
                )

        def square(k, c0, c1):
            if k not in sq_tiles:
                sq_tiles[k] = acc if k == 0 else work.tile([P, V], F32, name=f"sq{k}", tag="sq", bufs=5)
            nc.scalar.activation(
                out=sq_tiles[k][:, c0:c1], in_=y_tiles[k, c0][:], func=ACT.Square, scale=a_sb[:, k : k + 1]
            )

        def accumulate(k, c0, c1):
            nc.vector.tensor_tensor(out=acc[:, c0:c1], in0=acc[:, c0:c1], in1=sq_tiles[k][:, c0:c1], op=ALU.add)

        def contrast_vector(k, c0, c1):
            w = work.tile([P, c1 - c0], F32, name=f"wv{k}_{c0}", tag="wv", bufs=5)
            nc.vector.tensor_scalar(
                out=w[:], in0=y_tiles[k, c0][:], scalar1=a_sb[:, k : k + 1], scalar2=None, op0=ALU.mult
            )
            nc.sync.dma_start(out=out_0[P * k : P * (k + 1), c0:c1], in_=w[:])

        def stage2(k):
            w = work.tile([P, V], F32, name=f"w{k}", tag="w", bufs=4)
            for c0, c1 in halves:
                product(k, c0, c1)
                square(k, c0, c1)
                nc.scalar.activation(out=w[:, c0:c1], in_=y_tiles[k, c0][:], func=ACT.Copy, scale=a_sb[:, k : k + 1])
            nc.sync.dma_start(out=out_0[P * k : P * (k + 1), :], in_=w[:])

        def stage2_half(k, c0, c1):
            product(k, c0, c1)
            square(k, c0, c1)
            w = work.tile([P, c1 - c0], F32, name=f"wh{k}_{c0}", tag="wv", bufs=5)
            nc.scalar.activation(out=w[:], in_=y_tiles[k, c0][:], func=ACT.Copy, scale=a_sb[:, k : k + 1])
            nc.sync.dma_start(out=out_0[P * k : P * (k + 1), c0:c1], in_=w[:])

        def add_both(k):
            for c0, c1 in halves:
                accumulate(k, c0, c1)

        def finish(c0, c1, sources):
            ps = psum.tile([P, c1 - c0], F32, name=f"stat{c0}", tag="p", bufs=4)
            for i, s in enumerate(sources):
                nc.tensor.matmul(
                    out=ps[:], lhsT=ones[:], rhs=s[:, c0:c1], start=(i == 0), stop=(i == len(sources) - 1)
                )
            return ps

        def store_stat(c0, c1, ps):
            nc.vector.tensor_tensor(out=stat_sb[:, c0:c1], in0=ps[0:1, :], in1=r_sb[:, c0:c1], op=ALU.mult)
            nc.sync.dma_start(out=out_1.unsqueeze(0)[:, c0:c1], in_=stat_sb[:, c0:c1])

        units = [(c, g) for c in range(len(CHUNKS)) for g in range(GROUPS)]
        for g in range(GROUPS):
            permute(g)
            stage1(*units[g])
        for i in range(len(units)):
            if i + 4 < len(units):
                stage1(*units[i + 4])
            if i == 3:
                nc.vector.tensor_copy(out=a_sb[:], in_=a_bf[:])
            if i == 8:
                stage2(0)
                stage2(1)
            scale_by_u(*units[i])
            if i:
                quantize(*units[i - 1])
            if i >= 9:
                add_both(i - 8)
                stage2(i - 7)
        quantize(*units[-1])
        stage2(5)
        add_both(4)
        add_both(5)
        product(6, 0, 512)
        square(6, 0, 512)
        accumulate(6, 0, 512)
        contrast_vector(6, 0, 512)
        product(7, 0, 512)
        square(7, 0, 512)
        accumulate(7, 0, 512)
        contrast_vector(7, 0, 512)
        product(6, 512, 1024)
        square(6, 512, 1024)
        accumulate(6, 512, 1024)
        contrast_vector(6, 512, 1024)
        for c0, c1 in ((512, 768), (768, 1024)):
            product(7, c0, c1)
            square(7, c0, c1)
            accumulate(7, c0, c1)
            contrast_vector(7, c0, c1)
        ends = [(0, 512), (512, 768), (768, 1024)]
        sums = [finish(c0, c1, [acc]) for c0, c1 in ends]
        for (c0, c1), ps in zip(ends, sums):
            store_stat(c0, c1, ps)
